import numpy as np, ml_dtypes
CORES = [12,28,44,60,3,19,35,51]
N = 8
import mx_ref
NC = 128
BF = ml_dtypes.bfloat16
def setup_inputs(rng):
    def f(*shape):
        return mx_ref.flush((rng.standard_normal(shape, dtype=np.float32) * np.exp2(rng.integers(-2, 3, shape[:-1] + (1,)))).astype(BF))
    return {"w": f(N, 128, N * 512), "x": f(N, 128, 4 * NC)}
def setup_inputs_blocks(rng):
    d = setup_inputs(rng)
    for k in ("w", "x"): d[k] = mx_ref.spread(d[k], rng, 2)
    return d
def setup_inputs_wide(rng):
    d = setup_inputs(rng)
    for k in ("w", "x"): d[k] = mx_ref.flush((d[k].astype(np.float32) * np.exp2(rng.integers(-8, 9, (N, 1, 1))).astype(np.float32)).astype(BF))
    return d
def setup_inputs_zeros(rng):
    d = setup_inputs(rng); v = d["x"].reshape(N, 128, -1, 4).copy()
    v[np.broadcast_to((rng.random((N, 1, v.shape[2], 1)) < 0.33), v.shape)] = 0
    d["x"] = v.reshape(d["x"].shape)
    return d
def reference(w, x):
    QX = [mx_ref.quantize(x[j]) for j in range(N)]
    y = np.zeros((N, 128, NC), np.float32)
    for r in range(N):
        for j in range(N):
            p = mx_ref.matmul(mx_ref.quantize(w[r][:, 512 * j:512 * j + 512]), QX[j])
            y[r] = p if j == 0 else y[r] + p
    return {"y": y}

from concourse.bass import DstId, RemoteDMATransfer
from concourse.mybir import dt

N = 8
NC = 128
NCORES = 64

SCRATCH = {
    "xb": ("sbuf", [128, 4 * NC], "bfloat16"),
    "wb": ("sbuf", [128, 4 * NC * N], "bfloat16"),
    "xc": ("sbuf", [128, NC * N], "float8_e4m3fn_x4"),
    "xp": ("sbuf", [128, NC * N], "uint8"),
    "wc": ("sbuf", [128, NC * N], "float8_e4m3fn_x4"),
    "wp": ("sbuf", [128, NC * N], "uint8"),
    "acc": ("psum", [128, 512], "float32"),
    "yb": ("sbuf", [128, NC], "float32"),
}
SEMAPHORES = (["xl", "xq", "wl0", "wl1", "hc", "hp", "sent", "mm", "cp", "st"]
              + ["wq%d" % j for j in range(N)] + ["s%d" % j for j in range(N)])


def count(mask):
    return bin(mask).count("1")


def lanes(topo, src, dsts):
    m = topo.mask(src, dsts[0])
    for d in dsts[1:]:
        m &= topo.mask(src, d)
    return m


def route(T, topo, j):
    src = T.cores[j]
    here = topo.chip(src)
    after = [T.cores[(j + k) % N] for k in range(1, N)]
    direct = [d for d in after if topo.same_plane(here, topo.chip(d))]
    across = sorted(d for d in after if d not in direct)
    across.sort(key=T.rank_of)
    first = [i for i, d in enumerate(across) if topo.mates(here, topo.chip(d))]
    if first:
        across = across[first[0]:] + across[:first[0]]
    owners = [h for h in range(NCORES)
              if topo.chip(h) == here and T.rank_of(h) is None and all(topo.may_write(h, d) for d in across)]
    near = [h for h in owners if topo.die(h) == topo.die(src)]
    far = [h for h in owners if topo.die(h) != topo.die(src)]
    half = len(across) // 2
    code_fw = [(near[0], across[half:]), (far[0], across[:half])]
    plane_fw = [((near[1:] + far[1:])[0], across)]
    return direct, code_fw, plane_fw


def send(g, T, topo, parts, local_sem):
    transfers = []
    for mask, dsts, view, sem in parts:
        ids = []
        for d in dsts:
            rid, pid, ring = topo.addr(d)
            ids.append(DstId(rid=rid, pnc=pid))
        transfers.append(RemoteDMATransfer(dst_ids=ids, dma_engine_mask=mask, remote_sem=sem,
                                           srcs=[view], dsts=[view for d in dsts]))
    g.remote_dma_fused(transfers, local_sem=local_sem)
    return sum(count(p[0]) for p in parts)


def rank_program(g, core, T, topo):
    sem = T.sem
    routes = [route(T, topo, j) for j in range(N)]

    def codes(j):
        return T.xc[:, NC * j:NC * (j + 1)].bitcast(dt.uint8)

    def plane(j):
        return T.xp[:, NC * j:NC * (j + 1)]

    rank = T.rank_of(core)
    if rank is None:
        left = 0
        for j in range(N):
            direct, code_fw, plane_fw = routes[j]
            src = T.cores[j]
            fed = lanes(topo, src, [h for h, dsts in code_fw + plane_fw]) & ~lanes(topo, src, direct)
            for fws, landed, view in ((code_fw, sem.hc, codes(j)), (plane_fw, sem.hp, plane(j))):
                for h, dsts in fws:
                    if h == core:
                        g.wait_ge(landed, count(fed))
                        left += send(g, T, topo, [(lanes(topo, core, dsts), dsts, view, sem["s%d" % j])], sem.sent)
        if left:
            g.wait_ge(sem.sent, left)
        return

    expect = {}
    for j in range(N):
        if j == rank:
            continue
        direct, code_fw, plane_fw = routes[j]
        if core in direct:
            expect[j] = ((0, direct.index(core), 0), 2 * count(lanes(topo, T.cores[j], direct)))
        else:
            got, key = 0, [1]
            for h, dsts in code_fw + plane_fw:
                if core in dsts:
                    got += count(lanes(topo, h, dsts))
                    key.append(dsts.index(core))
            expect[j] = (tuple(key), got)
    order = [rank] + sorted(expect, key=lambda j: expect[j][0])

    g.sync.dma_start(T.xb[:], T.x[:]).then_inc(sem.xl, 16)
    halves = [rank // (N // 2), 1 - rank // (N // 2)]
    wide = 4 * NC * (N // 2)
    for h in halves:
        g.sync.dma_start(T.wb[:, wide * h:wide * (h + 1)], T.w[:, wide * h:wide * (h + 1)]).then_inc(sem["wl%d" % h], 16)

    g.vector.wait_ge(sem.xl, 16)
    g.vector.quantize_mx(T.xc[:, NC * rank:NC * (rank + 1)], plane(rank), T.xb[:]).then_inc(sem.xq, 1)
    for h in halves:
        g.vector.wait_ge(sem["wl%d" % h], 16)
        for j in order:
            if j // (N // 2) == h:
                g.vector.quantize_mx(T.wc[:, NC * j:NC * (j + 1)], T.wp[:, NC * j:NC * (j + 1)],
                                     T.wb[:, 4 * NC * j:4 * NC * (j + 1)]).then_inc(sem["wq%d" % j], 1)

    direct, code_fw, plane_fw = routes[rank]
    out = lanes(topo, core, direct)
    fed = lanes(topo, core, [h for h, dsts in code_fw + plane_fw]) & ~out
    mine = sem["s%d" % rank]
    g.wait_ge(sem.xq, 1)
    left = send(g, T, topo, [(fed, [h for h, dsts in code_fw], codes(rank), sem.hc),
                             (out, direct, codes(rank), mine)], sem.sent)
    left += send(g, T, topo, [(fed, [h for h, dsts in plane_fw], plane(rank), sem.hp),
                              (out, direct, plane(rank), mine)], sem.sent)

    for i, j in enumerate(order):
        if j == rank:
            g.tensor.wait_ge(sem.xq, 1)
        else:
            g.tensor.wait_ge(sem["s%d" % j], expect[j][1])
        g.tensor.wait_ge(sem["wq%d" % j], 1)
        mm = g.tensor.matmul_mx(T.acc[:, 0:NC], T.wc[:, NC * j:NC * (j + 1)], T.wp[:, NC * j:NC * (j + 1)],
                                T.xc[:, NC * j:NC * (j + 1)], plane(j), i == 0, i == N - 1)
    mm.then_inc(sem.mm, 1)

    g.vector.wait_ge(sem.mm, 1)
    g.vector.tensor_copy(T.yb[:], T.acc[:, 0:NC]).then_inc(sem.cp, 1)
    g.sync.wait_ge(sem.cp, 1)
    g.sync.dma_start(T.y[:], T.yb[:]).then_inc(sem.st, 16)
    g.sync.wait_ge(sem.st, 16)
    g.wait_ge(sem.sent, left)
